import numpy as np
import ml_dtypes


def mxq(x, axis, fmt="e4m3"):
    dtype, down = {"e4m3": (ml_dtypes.float8_e4m3fn, 7), "e5m2": (ml_dtypes.float8_e5m2, 14)}[fmt]
    v = np.moveaxis(np.asarray(x, np.float32).astype(ml_dtypes.bfloat16).astype(np.float64), axis, -1)
    blocks = v.reshape(v.shape[:-1] + (-1, 32))
    amax = np.abs(blocks).max(-1, keepdims=True)
    byte = np.maximum(np.where(amax > 0, np.frexp(amax)[1] - 1 + 127, 0) - down, 1)
    scale = np.exp2(byte - 127.0)
    codes = (blocks / scale).astype(np.float32).astype(dtype).astype(np.float64)
    return np.moveaxis((codes * scale).reshape(v.shape), -1, axis)


WIDE = False


def mx_kscale(k):
    if not WIDE:
        return np.ones(k)
    levels = np.array([10, -10, 5, -5, 0])
    if k % 512:
        return np.exp2(np.random.permutation(np.resize(levels, k // 32))).repeat(32)
    a = np.empty((k // 512, 16))
    for p in range(k // 512):
        a[p, :8] = np.random.permutation(np.resize(levels, 8))
        for g in range(8):
            far = levels[np.abs(levels - a[p, g]) >= 10]
            a[p, g + 8] = far[np.random.randint(len(far))]
    return np.exp2(a.ravel()).repeat(32)


def f64(x):
    return np.asarray(x).astype(np.float64)


def striped(idx):
    return np.tile(idx.reshape(-1, 16).T, (8, 1)).astype(np.uint16)


def unstriped(offs):
    return offs[:16].T.reshape(-1).astype(np.int64)


def striped8(idx):
    return np.concatenate([x.reshape(-1, 16).T for x in idx]).astype(np.uint16)


def runs(offs, k):
    lists = np.stack([offs[16 * r : 16 * r + 16].T.reshape(-1) for r in range(8)]).astype(np.int64)
    return lists[np.arange(k) % 512 // 64]


def pack_weight(w):
    k, n = w.shape
    w = f64(np.asarray(w, np.float32).astype(ml_dtypes.bfloat16)).reshape(k // 32, 32, n)
    amax = np.abs(w).max(1)
    byte = np.clip(np.where(amax > 0, np.frexp(amax)[1] - 1 + 127 - 7, 1), 1, 254)
    scaled = (w * np.exp2(127.0 - byte)[:, None, :]).reshape(k, n).astype(np.float32)
    words = np.ascontiguousarray(scaled.reshape(k // 512, 128, 4, n).transpose(0, 1, 3, 2)).astype(ml_dtypes.float8_e4m3fn).view(np.uint8)
    return words, np.ascontiguousarray(byte.astype(np.uint8).reshape(k // 512, 16, n))


def unpack_weight(words, scales):
    g, p, n, _ = words.shape
    vals = np.ascontiguousarray(words).view(ml_dtypes.float8_e4m3fn).astype(np.float64) * np.repeat(np.exp2(scales.astype(np.float64) - 127.0), 8, axis=1)[..., None]
    return vals.transpose(0, 1, 3, 2).reshape(g * 512, n)

def planes(y):
    n, m = y.shape
    v = y.astype(np.float32).astype(ml_dtypes.bfloat16).astype(np.float64).reshape(n // 32, 32, m)
    top = np.abs(v).max(1)
    byte = np.clip(np.where(top > 0, np.frexp(top)[1] - 1 + 127 - 7, 1), 1, 254)
    codes = (v * np.exp2(127.0 - byte)[:, None, :]).reshape(n, m).astype(np.float32).astype(ml_dtypes.float8_e4m3fn).view(np.uint8)
    words = codes.reshape(n // 512, 128, 4, m).transpose(0, 1, 3, 2)
    return np.ascontiguousarray(words), np.ascontiguousarray(byte.astype(np.uint8).reshape(n // 512, 16, m))


K, T, S, N, H, W, C = 512, 2048, 512, 512, 512, 256, 512


def setup_inputs():
    n = np.random.standard_normal
    s = mx_kscale(K)[:, None]
    u = mx_kscale(S)
    packed_xT = pack_weight(n((K, T)) * s)
    packed_w1 = pack_weight(n((K, H)) / np.sqrt(K) / s)
    packed_w2 = pack_weight(n((H, N)) / np.sqrt(H) / u[:, None])
    perm = np.stack([np.random.permutation(S) for _ in range(8)])
    return {
        "x_words": packed_xT[0],
        "x_scales": packed_xT[1],
        "w1_words": packed_w1[0],
        "w1_scales": packed_w1[1],
        "gn": (np.random.uniform(0.5, 1.5, (H, 1)) * u[:, None]).astype(np.float32),
        "w2_words": packed_w2[0],
        "w2_scales": packed_w2[1],
        "gs": (np.random.uniform(0.5, 1.5, (K, 1)) / s).astype(np.float32),
        "offs": striped(np.random.permutation(T)[:S]),
        "n1": striped8(np.stack([np.random.permutation(S) for _ in range(8)])),
        "n2": striped8(perm[:, :W]),
        "n3": striped8(perm[:, W:]),
        "cand": striped(np.random.permutation(T)[:C]),
        "n4": striped8(np.stack([np.random.permutation(S)[:W] for _ in range(8)])),
        "n5": striped8(np.stack([np.random.permutation(S)[:W] for _ in range(8)])),
    }


def reference(x_words, x_scales, w1_words, w1_scales, gn, w2_words, w2_scales, gs, offs, n1, n2, n3, cand, n4, n5):
    x_cand = unpack_weight(x_words, x_scales)[:, unstriped(cand)]
    xq = unpack_weight(x_words, x_scales)[:, unstriped(offs)]
    y = unpack_weight(w1_words, w1_scales).T @ xq
    pa = y[np.arange(H)[:, None], runs(n2, H)]
    pb = y[np.arange(H)[:, None], runs(n3, H)]
    rb = np.maximum(0.5 * pa, pb)
    ra = pb - pa
    ds = np.zeros((H, S))
    ds[np.arange(H)[:, None], runs(n2, H)] = ra
    dt = ds.copy()
    dt[np.arange(H)[:, None], runs(n3, H)] = rb
    z2 = f64(gs) * dt
    b = 0.0625 * ((x_cand.T @ mxq(z2, 0, "e4m3")))
    z = f64(gn) * (np.maximum(y, y[np.arange(H)[:, None], runs(n1, H)]))
    a = unpack_weight(w2_words, w2_scales).T @ mxq(z, 0, "e4m3")
    ra2 = b[np.arange(C)[:, None], runs(n5, C)] - (0.5 * (a[np.arange(N)[:, None], runs(n4, N)]))
    out = a.copy()
    out[np.arange(C)[:, None], runs(n4, C)] = ra2
    return (out,) + planes(out)

@@ -1,0 +1,247 @@
+from contextlib import ExitStack
+
+import concourse.mybir as mybir
+
+F32 = mybir.dt.float32
+BF16 = mybir.dt.bfloat16
+I32 = mybir.dt.int32
+U32 = mybir.dt.uint32
+U16 = mybir.dt.uint16
+U8 = mybir.dt.uint8
+FP8X4 = mybir.dt.float8_e4m3fn_x4
+ALU = mybir.AluOpType
+COPY = mybir.ActivationFunctionType.Copy
+
+P = 128
+PACK = 4
+T = 2048
+S = 512
+W = 256
+QUADS = 4
+SPLIT = 320
+
+FLOPS = 3 * 2 * 512 * 512 * 512
+
+
+def tile_picked_fkcdputbbiglift_none_po_kernel(
+    tc, x_words, x_scales, w1_words, w1_scales, gn, w2_words, w2_scales, gs,
+    offs, n1, n2, n3, cand, n4, n5, out_0, out_1, out_2,
+):
+    nc = tc.nc
+    with ExitStack() as ctx:
+        keep = ctx.enter_context(tc.tile_pool(name="keep", bufs=1))
+        psum = ctx.enter_context(tc.psum_pool(name="psum", bufs=1))
+
+        def sb(name, shape, dtype):
+            return keep.tile(shape, dtype, name=name, align_bytes=64)
+
+        def load_list(name, src):
+            tile = sb(name, list(src.shape), U16)
+            nc.sync.dma_start(tile[:], src)
+            return tile
+
+        def load_words(name, src, cols):
+            tile = sb(name, [P, cols], I32)
+            nc.sync.dma_start(tile[:], src[0].rearrange("p c r -> p (c r)").bitcast(I32))
+            return tile
+
+        def load_scale_rows(tile, src, queues):
+            for q in range(QUADS):
+                queues[q].dma_start(tile[32 * q : 32 * q + 4, :].bitcast(I32), src[0, 4 * q : 4 * q + 4, :].bitcast(I32))
+
+        def deal(name, src, dtype):
+            tile = sb(name, [P, S], dtype)
+            nc.vector.tensor_copy(
+                out=tile[:].rearrange("p (t m) -> p t m", t=PACK),
+                in_=src.rearrange("p (m t) -> p t m", t=PACK),
+            )
+            return tile
+
+        def product(bank, lhs_words, lhs_scales, rhs_words, rhs_scales, t):
+            cols = slice(P * t, P * (t + 1))
+            nc.tensor.matmul_mx(
+                out=bank[:],
+                lhsT=lhs_words[:, cols].bitcast(FP8X4), lhsT_scale=lhs_scales[:, cols],
+                rhs=rhs_words[:].bitcast(FP8X4), rhs_scale=rhs_scales[:],
+                start=True, stop=True,
+            )
+
+        def quantise(name, woven):
+            words = sb(name + "_words", [P, S], I32)
+            scales = sb(name + "_scales", [P, S], U8)
+            nc.vector.quantize_mx(out=words[:].bitcast(FP8X4), scales=scales[:], in_=woven[:])
+            return words, scales
+
+        def weave(engine_copy, woven, planes, lo, hi):
+            engine_copy(
+                woven[:, PACK * lo : PACK * hi].rearrange("p (c i t) -> p c t i", i=4, t=PACK),
+                planes[:, :, lo:hi].rearrange("p t (c i) -> p c t i", i=4),
+            )
+
+        def weave_and_quantise(name, planes):
+            woven = sb(name + "_woven", [P, PACK * S], BF16)
+            words = sb(name + "_words", [P, S], I32)
+            scales = sb(name + "_scales", [P, S], U8)
+            weave(nc.scalar.copy, woven, planes, SPLIT, S)
+            weave(nc.vector.tensor_copy, woven, planes, 0, W)
+            weave(nc.vector.tensor_copy, woven, planes, W, SPLIT)
+            for h in range(2):
+                nc.vector.quantize_mx(
+                    out=words[:, W * h : W * (h + 1)].bitcast(FP8X4), scales=scales[:, W * h : W * (h + 1)],
+                    in_=woven[:, PACK * W * h : PACK * W * (h + 1)],
+                )
+            return words, scales
+
+        def woven_view(tile):
+            return tile[:].rearrange("p (c i t) -> p c t i", i=4, t=PACK)
+
+        def planes_view(tile):
+            return tile[:].rearrange("p t (c i) -> p c t i", i=4)
+
+        xs = sb("xs", [P, T], U8)
+        nc.gpsimd.memset(xs[:].bitcast(I32), 0)
+        ws_raw = sb("ws_raw", [P, S], U8)
+        nc.gpsimd.memset(ws_raw[:].bitcast(I32), 0)
+
+        offs_l = load_list("offs_l", offs)
+        cand_l = load_list("cand_l", cand)
+        xw = load_words("xw", x_words, T)
+        w1w_raw = load_words("ww_raw", w1_words, S)
+        load_scale_rows(xs, x_scales, [nc.scalar] * QUADS)
+        load_scale_rows(ws_raw, w1_scales, [nc.scalar, nc.scalar, nc.gpsimd, nc.gpsimd])
+        n2_l = load_list("n2_l", n2)
+        n3_l = load_list("n3_l", n3)
+        n1_l = load_list("n1_l", n1)
+        gs_c = sb("gs_c", [P, PACK], F32)
+        nc.sync.dma_start(gs_c[:], gs.rearrange("(p t) o -> p (t o)", t=PACK))
+        gn_c = sb("gn_c", [P, PACK], F32)
+        nc.sync.dma_start(gn_c[:], gn.rearrange("(p t) o -> p (t o)", t=PACK))
+        n4_l = load_list("n4_l", n4)
+        n5_l = load_list("n5_l", n5)
+
+        xq_s = sb("xq_s", [P, S], U8)
+        nc.vector.tensor_copy(xq_s[:], xs[:].indirect(offs_l[:]))
+        xc_s_raw = sb("xc_s_raw", [P, S], U8)
+        nc.vector.tensor_copy(xc_s_raw[:], xs[:].indirect(cand_l[:]))
+        xq_w = sb("xq_w", [P, S], U32)
+        nc.vector.tensor_copy(xq_w[:], xw[:].bitcast(U32).indirect(offs_l[:]))
+        w1w = deal("w1w", w1w_raw[:], I32)
+        w1s = deal("w1s", ws_raw[:], U8)
+
+        banks_y = [psum.tile([P, S], F32, name=f"bank_lo{t}") for t in range(PACK)]
+        for t in range(PACK):
+            product(banks_y[t], w1w, w1s, xq_w, xq_s, t)
+
+        w2w_raw = load_words("ww_raw", w2_words, S)
+        load_scale_rows(ws_raw, w2_scales, [nc.sync] * QUADS)
+
+        xc_w_raw = sb("xc_w_raw", [P, S], U32)
+        nc.vector.tensor_copy(xc_w_raw[:], xw[:].bitcast(U32).indirect(cand_l[:]))
+        xc_w = deal("xc_w", xc_w_raw[:].bitcast(I32), I32)
+        xc_s = deal("xc_s", xc_s_raw[:], U8)
+
+        z_planes = sb("z_planes", [P, PACK, S], BF16)
+        z2_planes = sb("z2_planes", [P, PACK, S], BF16)
+        y = [sb(f"y{t}", [P, S], F32) for t in range(PACK)]
+        dt = [sb(f"dt{t}", [P, S], F32) for t in range(PACK)]
+        larger = [sb(f"larger{t}", [P, S], F32) for t in range(PACK)]
+
+        def fetch_y(t):
+            nc.scalar.copy(y[t][:], banks_y[t][:])
+
+        def pair_up(t):
+            neg_pa = sb(f"neg_pa{t}", [P, W], F32)
+            nc.scalar.activation(neg_pa[:], y[t][:].indirect(n2_l[:]), COPY, scale=-1.0)
+            pb = sb(f"pb{t}", [P, W], F32)
+            nc.scalar.activation(pb[:], y[t][:].indirect(n3_l[:]), COPY)
+            rb = sb(f"rb{t}", [P, W], F32)
+            nc.vector.scalar_tensor_tensor(rb[:], neg_pa[:], -0.5, pb[:], ALU.mult, ALU.max)
+            nc.vector.tensor_tensor(dt[t][:].indirect(n2_l[:]), pb[:], neg_pa[:], ALU.add)
+            nc.vector.tensor_copy(dt[t][:].indirect(n3_l[:]), rb[:])
+
+        def neighbour_max(t):
+            other = sb(f"other{t}", [P, S], F32)
+            for h in range(2):
+                nc.scalar.activation(other[:, W * h : W * (h + 1)], y[t][:].indirect(n1_l[:, 16 * h : 16 * (h + 1)]), COPY)
+            nc.vector.tensor_tensor(larger[t][:], y[t][:], other[:], ALU.max)
+
+        def round_z(t):
+            nc.scalar.activation(z_planes[:, t, :], larger[t][:], COPY, scale=gn_c[:, t : t + 1])
+
+        def round_z2(t):
+            nc.scalar.activation(z2_planes[:, t, :], dt[t][:], COPY, scale=gs_c[:, t : t + 1])
+
+        fetch_y(0)
+        pair_up(0)
+        fetch_y(1)
+        neighbour_max(0)
+        pair_up(1)
+        fetch_y(2)
+        neighbour_max(1)
+        fetch_y(3)
+        neighbour_max(2)
+        pair_up(2)
+        neighbour_max(3)
+        pair_up(3)
+        w2w = deal("w2w", w2w_raw[:], I32)
+        w2s = deal("w2s", ws_raw[:], U8)
+        round_z(0)
+        round_z(1)
+        round_z(2)
+        round_z2(0)
+        round_z2(1)
+        round_z(3)
+
+        z_woven = sb("z_woven", [P, PACK * S], BF16)
+        nc.scalar.copy(woven_view(z_woven), planes_view(z_planes))
+        round_z2(2)
+        round_z2(3)
+        z_w, z_s = quantise("z", z_woven)
+        banks_a = [psum.tile([P, S], F32, name=f"bank_hi{t}") for t in range(PACK)]
+        for t in range(PACK):
+            product(banks_a[t], w2w, w2s, z_w, z_s, t)
+
+        z2_w, z2_s = weave_and_quantise("z2", z2_planes)
+        banks_b = [psum.tile([P, S], F32, name=f"bank_lo{t}") for t in range(PACK)]
+        for t in range(PACK):
+            product(banks_b[t], xc_w, xc_s, z2_w, z2_s, t)
+
+        out_rows = out_0.rearrange("(p t) j -> p t j", t=PACK)
+        out_planes = sb("out_planes", [P, PACK, S], BF16)
+        res = [sb(f"res{t}", [P, S], F32) for t in range(PACK)]
+        a_part = [sb(f"a_part{t}", [P, W], F32) for t in range(PACK)]
+
+        def fetch_a(t):
+            nc.scalar.copy(res[t][:], banks_a[t][:])
+            nc.scalar.activation(a_part[t][:], res[t][:].indirect(n4_l[:]), COPY, scale=-0.5)
+
+        def put(t, on_vector):
+            b = sb(f"b{t}", [P, S], F32)
+            b_part = sb(f"b_part{t}", [P, W], F32)
+            if on_vector:
+                nc.vector.tensor_scalar(b[:], banks_b[t][:], 0.0625, None, ALU.mult)
+                nc.vector.tensor_copy(b_part[:], b[:].indirect(n5_l[:]))
+            else:
+                nc.scalar.activation(b[:], banks_b[t][:], COPY, scale=0.0625)
+                nc.scalar.activation(b_part[:], b[:].indirect(n5_l[:]), COPY)
+            nc.vector.tensor_tensor(res[t][:].indirect(n4_l[:]), b_part[:], a_part[t][:], ALU.add)
+            nc.sync.dma_start(out_rows[:, t, :], res[t][:])
+
+        fetch_a(0)
+        fetch_a(1)
+        put(0, True)
+        put(1, False)
+        fetch_a(2)
+        put(2, False)
+        fetch_a(3)
+        put(3, False)
+        for t in range(PACK - 1):
+            nc.scalar.copy(out_planes[:, t, :], res[t][:])
+        nc.vector.tensor_copy(out_planes[:, PACK - 1, :], res[PACK - 1][:])
+
+        o_w, o_s = weave_and_quantise("o", out_planes)
+        out_words = out_1[0].rearrange("p c r -> p (c r)").bitcast(I32)
+        for h in range(2):
+            nc.sync.dma_start(out_words[:, W * h : W * (h + 1)], o_w[:, W * h : W * (h + 1)])
+        for q in range(QUADS):
+            nc.scalar.dma_start(out_2[0, 4 * q : 4 * q + 4, :].bitcast(I32), o_s[32 * q : 32 * q + 4, :].bitcast(I32))

@@ -19,6 +19,8 @@ S = 512
 W = 256
 QUADS = 4
 SPLIT = 320
+Z_SPLIT = 192
+HALVES = [slice(0, W), slice(W, S)]
 
 FLOPS = 3 * 2 * 512 * 512 * 512
 
@@ -30,10 +32,11 @@ def tile_picked_fkcdputbbiglift_none_po_kernel(
     nc = tc.nc
     with ExitStack() as ctx:
         keep = ctx.enter_context(tc.tile_pool(name="keep", bufs=1))
+        reuse = ctx.enter_context(tc.tile_pool(name="reuse", bufs=1))
         psum = ctx.enter_context(tc.psum_pool(name="psum", bufs=1))
 
-        def sb(name, shape, dtype):
-            return keep.tile(shape, dtype, name=name, align_bytes=64)
+        def sb(name, shape, dtype, tag=None):
+            return keep.tile(shape, dtype, name=name, tag=tag or name, align_bytes=64)
 
         def load_list(name, src):
             tile = sb(name, list(src.shape), U16)
@@ -49,20 +52,19 @@ def tile_picked_fkcdputbbiglift_none_po_kernel(
             for q in range(QUADS):
                 queues[q].dma_start(tile[32 * q : 32 * q + 4, :].bitcast(I32), src[0, 4 * q : 4 * q + 4, :].bitcast(I32))
 
-        def deal(name, src, dtype):
-            tile = sb(name, [P, S], dtype)
-            nc.vector.tensor_copy(
+        def deal(engine, tile, src):
+            engine.tensor_copy(
                 out=tile[:].rearrange("p (t m) -> p t m", t=PACK),
                 in_=src.rearrange("p (m t) -> p t m", t=PACK),
             )
             return tile
 
-        def product(bank, lhs_words, lhs_scales, rhs_words, rhs_scales, t):
+        def product(bank, lhs_words, lhs_scales, rhs_words, rhs_scales, t, span=slice(0, S)):
             cols = slice(P * t, P * (t + 1))
             nc.tensor.matmul_mx(
                 out=bank[:],
                 lhsT=lhs_words[:, cols].bitcast(FP8X4), lhsT_scale=lhs_scales[:, cols],
-                rhs=rhs_words[:].bitcast(FP8X4), rhs_scale=rhs_scales[:],
+                rhs=rhs_words[:, span].bitcast(FP8X4), rhs_scale=rhs_scales[:, span],
                 start=True, stop=True,
             )
 
@@ -98,24 +100,31 @@ def tile_picked_fkcdputbbiglift_none_po_kernel(
         def planes_view(tile):
             return tile[:].rearrange("p t (c i) -> p c t i", i=4)
 
-        xs = sb("xs", [P, T], U8)
-        nc.gpsimd.memset(xs[:].bitcast(I32), 0)
-        ws_raw = sb("ws_raw", [P, S], U8)
-        nc.gpsimd.memset(ws_raw[:].bitcast(I32), 0)
+        w1s_raw = sb("w1s_raw", [P, S], U8)
+        nc.gpsimd.memset(w1s_raw[:].bitcast(I32), 0)
+        w2s_raw = sb("w2s_raw", [P, S], U8)
+        nc.gpsimd.memset(w2s_raw[:].bitcast(I32), 0)
 
         offs_l = load_list("offs_l", offs)
         cand_l = load_list("cand_l", cand)
+        xs = sb("xs", [P, T], U8)
+        for q in range(QUADS):
+            nc.sync.dma_start(
+                xs[32 * q : 32 * (q + 1), :].bitcast(I32),
+                x_scales[:, 4 * q : 4 * q + 4, :].bitcast(I32).to_broadcast([8, 4, T // 4]),
+            )
+        w1w_raw = load_words("w1w_raw", w1_words, S)
         xw = load_words("xw", x_words, T)
-        w1w_raw = load_words("ww_raw", w1_words, S)
-        load_scale_rows(xs, x_scales, [nc.scalar] * QUADS)
-        load_scale_rows(ws_raw, w1_scales, [nc.scalar, nc.scalar, nc.gpsimd, nc.gpsimd])
+        load_scale_rows(w1s_raw, w1_scales, [nc.sync] * QUADS)
         n2_l = load_list("n2_l", n2)
         n3_l = load_list("n3_l", n3)
         n1_l = load_list("n1_l", n1)
-        gs_c = sb("gs_c", [P, PACK], F32)
-        nc.sync.dma_start(gs_c[:], gs.rearrange("(p t) o -> p (t o)", t=PACK))
+        w2w_raw = load_words("w2w_raw", w2_words, S)
+        load_scale_rows(w2s_raw, w2_scales, [nc.sync] * QUADS)
         gn_c = sb("gn_c", [P, PACK], F32)
         nc.sync.dma_start(gn_c[:], gn.rearrange("(p t) o -> p (t o)", t=PACK))
+        gs_c = sb("gs_c", [P, PACK], F32)
+        nc.sync.dma_start(gs_c[:], gs.rearrange("(p t) o -> p (t o)", t=PACK))
         n4_l = load_list("n4_l", n4)
         n5_l = load_list("n5_l", n5)
 
@@ -124,45 +133,58 @@ def tile_picked_fkcdputbbiglift_none_po_kernel(
         xc_s_raw = sb("xc_s_raw", [P, S], U8)
         nc.vector.tensor_copy(xc_s_raw[:], xs[:].indirect(cand_l[:]))
         xq_w = sb("xq_w", [P, S], U32)
-        nc.vector.tensor_copy(xq_w[:], xw[:].bitcast(U32).indirect(offs_l[:]))
-        w1w = deal("w1w", w1w_raw[:], I32)
-        w1s = deal("w1s", ws_raw[:], U8)
+        for h in range(2):
+            nc.vector.tensor_copy(xq_w[:, HALVES[h]], xw[:].bitcast(U32).indirect(offs_l[:, 16 * h : 16 * (h + 1)]))
+        w1w = deal(nc.gpsimd, sb("w1w", [P, S], I32), w1w_raw[:])
+        w1s = deal(nc.gpsimd, sb("w1s", [P, S], U8), w1s_raw[:])
 
-        banks_y = [psum.tile([P, S], F32, name=f"bank_lo{t}") for t in range(PACK)]
-        for t in range(PACK):
+        y = [sb(f"y{t}", [P, S], F32) for t in range(PACK)]
+        for h in range(2):
+            bank = psum.tile([P, W], F32, name=f"y0_{h}", tag=f"bank{h}")
+            product(bank, w1w, w1s, xq_w, xq_s, 0, HALVES[h])
+            nc.scalar.copy(y[0][:, HALVES[h]], bank[:])
+        banks_y = {t: psum.tile([P, S], F32, name=f"y{t}_bank", tag=f"bank{t + 1}") for t in range(1, PACK)}
+        for t in range(1, PACK):
             product(banks_y[t], w1w, w1s, xq_w, xq_s, t)
-
-        w2w_raw = load_words("ww_raw", w2_words, S)
-        load_scale_rows(ws_raw, w2_scales, [nc.sync] * QUADS)
 
         xc_w_raw = sb("xc_w_raw", [P, S], U32)
         nc.vector.tensor_copy(xc_w_raw[:], xw[:].bitcast(U32).indirect(cand_l[:]))
-        xc_w = deal("xc_w", xc_w_raw[:].bitcast(I32), I32)
-        xc_s = deal("xc_s", xc_s_raw[:], U8)
+        w2w = deal(nc.gpsimd, sb("w2w", [P, S], I32), w2w_raw[:])
+        w2s = deal(nc.gpsimd, sb("w2s", [P, S], U8), w2s_raw[:])
 
         z_planes = sb("z_planes", [P, PACK, S], BF16)
         z2_planes = sb("z2_planes", [P, PACK, S], BF16)
-        y = [sb(f"y{t}", [P, S], F32) for t in range(PACK)]
         dt = [sb(f"dt{t}", [P, S], F32) for t in range(PACK)]
         larger = [sb(f"larger{t}", [P, S], F32) for t in range(PACK)]
+        neg_pa = sb("neg_pa", [P, PACK * W], F32)
+        pb = sb("pb", [P, PACK * W], F32)
+
+        def part(tile, t, count=1):
+            return tile[:, W * t : W * (t + count)]
 
         def fetch_y(t):
             nc.scalar.copy(y[t][:], banks_y[t][:])
 
-        def pair_up(t):
-            neg_pa = sb(f"neg_pa{t}", [P, W], F32)
-            nc.scalar.activation(neg_pa[:], y[t][:].indirect(n2_l[:]), COPY, scale=-1.0)
-            pb = sb(f"pb{t}", [P, W], F32)
-            nc.scalar.activation(pb[:], y[t][:].indirect(n3_l[:]), COPY)
-            rb = sb(f"rb{t}", [P, W], F32)
-            nc.vector.scalar_tensor_tensor(rb[:], neg_pa[:], -0.5, pb[:], ALU.mult, ALU.max)
-            nc.vector.tensor_tensor(dt[t][:].indirect(n2_l[:]), pb[:], neg_pa[:], ALU.add)
-            nc.vector.tensor_copy(dt[t][:].indirect(n3_l[:]), rb[:])
+        def fetch_pairs(t):
+            nc.scalar.activation(part(neg_pa, t), y[t][:].indirect(n2_l[:]), COPY, scale=-1.0)
+            if t == 0:
+                nc.vector.tensor_copy(part(pb, t), y[t][:].indirect(n3_l[:]))
+            else:
+                nc.scalar.activation(part(pb, t), y[t][:].indirect(n3_l[:]), COPY)
+
+        def put_difference(t):
+            nc.vector.tensor_tensor(dt[t][:].indirect(n2_l[:]), part(pb, t), part(neg_pa, t), ALU.add)
+
+        def pair_max(rb, t, count):
+            nc.vector.scalar_tensor_tensor(rb[:], part(neg_pa, t, count), -0.5, part(pb, t, count), ALU.mult, ALU.max)
+
+        def put_larger(t, rb):
+            nc.vector.tensor_copy(dt[t][:].indirect(n3_l[:]), rb)
 
         def neighbour_max(t):
             other = sb(f"other{t}", [P, S], F32)
             for h in range(2):
-                nc.scalar.activation(other[:, W * h : W * (h + 1)], y[t][:].indirect(n1_l[:, 16 * h : 16 * (h + 1)]), COPY)
+                nc.scalar.activation(other[:, HALVES[h]], y[t][:].indirect(n1_l[:, 16 * h : 16 * (h + 1)]), COPY)
             nc.vector.tensor_tensor(larger[t][:], y[t][:], other[:], ALU.max)
 
         def round_z(t):
@@ -171,70 +193,92 @@ def tile_picked_fkcdputbbiglift_none_po_kernel(
         def round_z2(t):
             nc.scalar.activation(z2_planes[:, t, :], dt[t][:], COPY, scale=gs_c[:, t : t + 1])
 
-        fetch_y(0)
-        pair_up(0)
+        fetch_pairs(0)
+        put_difference(0)
         fetch_y(1)
+        fetch_pairs(1)
+        rb01 = sb("rb01", [P, 2 * W], F32)
+        pair_max(rb01, 0, 2)
+        put_difference(1)
+        put_larger(0, part(rb01, 0))
+        put_larger(1, part(rb01, 1))
         neighbour_max(0)
-        pair_up(1)
         fetch_y(2)
         neighbour_max(1)
         fetch_y(3)
         neighbour_max(2)
-        pair_up(2)
+        fetch_pairs(2)
+        rb2 = sb("rb2", [P, W], F32)
+        pair_max(rb2, 2, 1)
+        put_difference(2)
         neighbour_max(3)
-        pair_up(3)
-        w2w = deal("w2w", w2w_raw[:], I32)
-        w2s = deal("w2s", ws_raw[:], U8)
-        round_z(0)
-        round_z(1)
-        round_z(2)
-        round_z2(0)
-        round_z2(1)
-        round_z(3)
+        fetch_pairs(3)
+        put_difference(3)
+        put_larger(2, rb2[:])
+        for t in range(PACK):
+            round_z(t)
 
-        z_woven = sb("z_woven", [P, PACK * S], BF16)
-        nc.scalar.copy(woven_view(z_woven), planes_view(z_planes))
-        round_z2(2)
-        round_z2(3)
+        z_woven = reuse.tile([P, PACK * S], BF16, name="z_woven", offset=0, align_bytes=64)
+        weave(nc.scalar.copy, z_woven, z_planes, Z_SPLIT, S)
+        weave(nc.vector.tensor_copy, z_woven, z_planes, 0, Z_SPLIT)
         z_w, z_s = quantise("z", z_woven)
-        banks_a = [psum.tile([P, S], F32, name=f"bank_hi{t}") for t in range(PACK)]
+        banks_a = [psum.tile([P, S], F32, name=f"a{t}_bank", tag=f"bank{(t + 5) % 8}") for t in range(PACK)]
         for t in range(PACK):
             product(banks_a[t], w2w, w2s, z_w, z_s, t)
-
-        z2_w, z2_s = weave_and_quantise("z2", z2_planes)
-        banks_b = [psum.tile([P, S], F32, name=f"bank_lo{t}") for t in range(PACK)]
-        for t in range(PACK):
-            product(banks_b[t], xc_w, xc_s, z2_w, z2_s, t)
+        rb3 = reuse.tile([P, W], F32, name="rb3", offset=0, align_bytes=64)
+        pair_max(rb3, 3, 1)
+        xc_w = deal(nc.vector, reuse.tile([P, S], I32, name="xc_w", offset=1024, align_bytes=64), xc_w_raw[:].bitcast(I32))
+        xc_s = deal(nc.vector, reuse.tile([P, S], U8, name="xc_s", offset=3072, align_bytes=64), xc_s_raw[:])
+        put_larger(3, rb3[:])
+        for t in range(PACK - 1):
+            round_z2(t)
 
         out_rows = out_0.rearrange("(p t) j -> p t j", t=PACK)
         out_planes = sb("out_planes", [P, PACK, S], BF16)
-        res = [sb(f"res{t}", [P, S], F32) for t in range(PACK)]
+        res = []
         a_part = [sb(f"a_part{t}", [P, W], F32) for t in range(PACK)]
 
         def fetch_a(t):
+            res.append(sb(f"res{t}", [P, S], F32, tag="b1" if t == 3 else None))
             nc.scalar.copy(res[t][:], banks_a[t][:])
             nc.scalar.activation(a_part[t][:], res[t][:].indirect(n4_l[:]), COPY, scale=-0.5)
 
-        def put(t, on_vector):
-            b = sb(f"b{t}", [P, S], F32)
-            b_part = sb(f"b_part{t}", [P, W], F32)
-            if on_vector:
-                nc.vector.tensor_scalar(b[:], banks_b[t][:], 0.0625, None, ALU.mult)
-                nc.vector.tensor_copy(b_part[:], b[:].indirect(n5_l[:]))
-            else:
-                nc.scalar.activation(b[:], banks_b[t][:], COPY, scale=0.0625)
-                nc.scalar.activation(b_part[:], b[:].indirect(n5_l[:]), COPY)
+        def put(t, b_part):
             nc.vector.tensor_tensor(res[t][:].indirect(n4_l[:]), b_part[:], a_part[t][:], ALU.add)
             nc.sync.dma_start(out_rows[:, t, :], res[t][:])
 
+        def fetch_b(t):
+            b = sb(f"b{t}", [P, S], F32)
+            b_part = sb(f"b_part{t}", [P, W], F32)
+            nc.scalar.activation(b[:], banks_b[t][:], COPY, scale=0.0625)
+            nc.scalar.activation(b_part[:], b[:].indirect(n5_l[:]), COPY)
+            return b_part
+
         fetch_a(0)
         fetch_a(1)
-        put(0, True)
-        put(1, False)
+        nc.vector.tensor_scalar(z2_planes[:, PACK - 1, :], dt[PACK - 1][:], gs_c[:, PACK - 1 : PACK], None, ALU.mult)
+        z2_w, z2_s = weave_and_quantise("z2", z2_planes)
         fetch_a(2)
-        put(2, False)
+
+        b0 = sb("b0", [P, S], F32)
+        for h in range(2):
+            bank = psum.tile([P, W], F32, name=f"b0_{h}", tag=f"bank{h + 1}")
+            product(bank, xc_w, xc_s, z2_w, z2_s, 0, HALVES[h])
+            if h == 0:
+                nc.scalar.activation(b0[:, HALVES[h]], bank[:], COPY, scale=0.0625)
+            else:
+                nc.vector.tensor_scalar(b0[:, HALVES[h]], bank[:], 0.0625, None, ALU.mult)
+        banks_b = {t: psum.tile([P, S], F32, name=f"b{t}_bank", tag=f"bank{t + 2}") for t in range(1, PACK)}
+        for t in range(1, PACK):
+            product(banks_b[t], xc_w, xc_s, z2_w, z2_s, t)
+        b_part0 = sb("b_part0", [P, W], F32)
+        nc.scalar.activation(b_part0[:, 0:128], b0[:].indirect(n5_l[:, 0:8]), COPY)
+        nc.vector.tensor_copy(b_part0[:, 128:256], b0[:].indirect(n5_l[:, 8:16]))
+        put(0, b_part0)
+        put(1, fetch_b(1))
+        put(2, fetch_b(2))
         fetch_a(3)
-        put(3, False)
+        put(3, fetch_b(3))
         for t in range(PACK - 1):
             nc.scalar.copy(out_planes[:, t, :], res[t][:])
         nc.vector.tensor_copy(out_planes[:, PACK - 1, :], res[PACK - 1][:])
@@ -242,6 +286,6 @@ def tile_picked_fkcdputbbiglift_none_po_kernel(
         o_w, o_s = weave_and_quantise("o", out_planes)
         out_words = out_1[0].rearrange("p c r -> p (c r)").bitcast(I32)
         for h in range(2):
-            nc.sync.dma_start(out_words[:, W * h : W * (h + 1)], o_w[:, W * h : W * (h + 1)])
+            nc.sync.dma_start(out_words[:, HALVES[h]], o_w[:, HALVES[h]])
         for q in range(QUADS):
             nc.scalar.dma_start(out_2[0, 4 * q : 4 * q + 4, :].bitcast(I32), o_s[32 * q : 32 * q + 4, :].bitcast(I32))

@@ -19,7 +19,6 @@ S = 512
 W = 256
 QUADS = 4
 SPLIT = 320
-Z_SPLIT = 192
 HALVES = [slice(0, W), slice(W, S)]
 
 FLOPS = 3 * 2 * 512 * 512 * 512
@@ -100,20 +99,17 @@ def tile_picked_fkcdputbbiglift_none_po_kernel(
         def planes_view(tile):
             return tile[:].rearrange("p t (c i) -> p c t i", i=4)
 
-        w1s_raw = sb("w1s_raw", [P, S], U8)
+        xs = sb("xs", [P, T], U8)
+        nc.gpsimd.memset(xs[:].bitcast(I32), 0)
+        w1s_raw = reuse.tile([P, S], U8, name="w1s_raw", offset=4096, align_bytes=64)
         nc.gpsimd.memset(w1s_raw[:].bitcast(I32), 0)
         w2s_raw = sb("w2s_raw", [P, S], U8)
         nc.gpsimd.memset(w2s_raw[:].bitcast(I32), 0)
 
         offs_l = load_list("offs_l", offs)
         cand_l = load_list("cand_l", cand)
-        xs = sb("xs", [P, T], U8)
-        for q in range(QUADS):
-            nc.sync.dma_start(
-                xs[32 * q : 32 * (q + 1), :].bitcast(I32),
-                x_scales[:, 4 * q : 4 * q + 4, :].bitcast(I32).to_broadcast([8, 4, T // 4]),
-            )
         w1w_raw = load_words("w1w_raw", w1_words, S)
+        load_scale_rows(xs, x_scales, [nc.sync] * QUADS)
         xw = load_words("xw", x_words, T)
         load_scale_rows(w1s_raw, w1_scales, [nc.sync] * QUADS)
         n2_l = load_list("n2_l", n2)
@@ -133,10 +129,10 @@ def tile_picked_fkcdputbbiglift_none_po_kernel(
         xc_s_raw = sb("xc_s_raw", [P, S], U8)
         nc.vector.tensor_copy(xc_s_raw[:], xs[:].indirect(cand_l[:]))
         xq_w = sb("xq_w", [P, S], U32)
+        w1w = deal(nc.vector, sb("w1w", [P, S], I32), w1w_raw[:])
+        w1s = deal(nc.vector, sb("w1s", [P, S], U8), w1s_raw[:])
         for h in range(2):
             nc.vector.tensor_copy(xq_w[:, HALVES[h]], xw[:].bitcast(U32).indirect(offs_l[:, 16 * h : 16 * (h + 1)]))
-        w1w = deal(nc.gpsimd, sb("w1w", [P, S], I32), w1w_raw[:])
-        w1s = deal(nc.gpsimd, sb("w1s", [P, S], U8), w1s_raw[:])
 
         y = [sb(f"y{t}", [P, S], F32) for t in range(PACK)]
         for h in range(2):
@@ -147,15 +143,15 @@ def tile_picked_fkcdputbbiglift_none_po_kernel(
         for t in range(1, PACK):
             product(banks_y[t], w1w, w1s, xq_w, xq_s, t)
 
-        xc_w_raw = sb("xc_w_raw", [P, S], U32)
+        xc_w_raw = reuse.tile([P, S], U32, name="xc_w_raw", offset=4096, align_bytes=64)
         nc.vector.tensor_copy(xc_w_raw[:], xw[:].bitcast(U32).indirect(cand_l[:]))
-        w2w = deal(nc.gpsimd, sb("w2w", [P, S], I32), w2w_raw[:])
-        w2s = deal(nc.gpsimd, sb("w2s", [P, S], U8), w2s_raw[:])
+        w2w = deal(nc.vector, sb("w2w", [P, S], I32), w2w_raw[:])
+        w2s = deal(nc.vector, sb("w2s", [P, S], U8), w2s_raw[:])
 
         z_planes = sb("z_planes", [P, PACK, S], BF16)
         z2_planes = sb("z2_planes", [P, PACK, S], BF16)
         dt = [sb(f"dt{t}", [P, S], F32) for t in range(PACK)]
-        larger = [sb(f"larger{t}", [P, S], F32) for t in range(PACK)]
+        larger = sb("larger", [P, PACK, S], F32)
         neg_pa = sb("neg_pa", [P, PACK * W], F32)
         pb = sb("pb", [P, PACK * W], F32)
 
@@ -185,10 +181,10 @@ def tile_picked_fkcdputbbiglift_none_po_kernel(
             other = sb(f"other{t}", [P, S], F32)
             for h in range(2):
                 nc.scalar.activation(other[:, HALVES[h]], y[t][:].indirect(n1_l[:, 16 * h : 16 * (h + 1)]), COPY)
-            nc.vector.tensor_tensor(larger[t][:], y[t][:], other[:], ALU.max)
+            nc.vector.tensor_tensor(larger[:, t, :], y[t][:], other[:], ALU.max)
 
         def round_z(t):
-            nc.scalar.activation(z_planes[:, t, :], larger[t][:], COPY, scale=gn_c[:, t : t + 1])
+            nc.scalar.activation(z_planes[:, t, :], larger[:, t, :], COPY, scale=gn_c[:, t : t + 1])
 
         def round_z2(t):
             nc.scalar.activation(z2_planes[:, t, :], dt[t][:], COPY, scale=gs_c[:, t : t + 1])
@@ -219,8 +215,7 @@ def tile_picked_fkcdputbbiglift_none_po_kernel(
             round_z(t)
 
         z_woven = reuse.tile([P, PACK * S], BF16, name="z_woven", offset=0, align_bytes=64)
-        weave(nc.scalar.copy, z_woven, z_planes, Z_SPLIT, S)
-        weave(nc.vector.tensor_copy, z_woven, z_planes, 0, Z_SPLIT)
+        weave(nc.scalar.copy, z_woven, z_planes, 0, S)
         z_w, z_s = quantise("z", z_woven)
         banks_a = [psum.tile([P, S], F32, name=f"a{t}_bank", tag=f"bank{(t + 5) % 8}") for t in range(PACK)]
         for t in range(PACK):
@@ -234,7 +229,7 @@ def tile_picked_fkcdputbbiglift_none_po_kernel(
             round_z2(t)
 
         out_rows = out_0.rearrange("(p t) j -> p t j", t=PACK)
-        out_planes = sb("out_planes", [P, PACK, S], BF16)
+        out_planes = sb("out_planes", [P, PACK, S], F32)
         res = []
         a_part = [sb(f"a_part{t}", [P, W], F32) for t in range(PACK)]
 
@@ -245,6 +240,8 @@ def tile_picked_fkcdputbbiglift_none_po_kernel(
 
         def put(t, b_part):
             nc.vector.tensor_tensor(res[t][:].indirect(n4_l[:]), b_part[:], a_part[t][:], ALU.add)
+            if t < 2:
+                nc.sync.dma_start(out_planes[:, t, :], res[t][:])
             nc.sync.dma_start(out_rows[:, t, :], res[t][:])
 
         def fetch_b(t):
@@ -256,7 +253,8 @@ def tile_picked_fkcdputbbiglift_none_po_kernel(
 
         fetch_a(0)
         fetch_a(1)
-        nc.vector.tensor_scalar(z2_planes[:, PACK - 1, :], dt[PACK - 1][:], gs_c[:, PACK - 1 : PACK], None, ALU.mult)
+        nc.vector.tensor_scalar(z2_planes[:, 3, 0:SPLIT], dt[3][:, 0:SPLIT], gs_c[:, 3:4], None, ALU.mult)
+        nc.scalar.activation(z2_planes[:, 3, SPLIT:S], dt[3][:, SPLIT:S], COPY, scale=gs_c[:, 3:4])
         z2_w, z2_s = weave_and_quantise("z2", z2_planes)
         fetch_a(2)
 
@@ -279,9 +277,9 @@ def tile_picked_fkcdputbbiglift_none_po_kernel(
         put(2, fetch_b(2))
         fetch_a(3)
         put(3, fetch_b(3))
-        for t in range(PACK - 1):
-            nc.scalar.copy(out_planes[:, t, :], res[t][:])
-        nc.vector.tensor_copy(out_planes[:, PACK - 1, :], res[PACK - 1][:])
+        nc.scalar.copy(out_planes[:, 2, :], res[2][:])
+        nc.vector.tensor_copy(out_planes[:, 3, 0:SPLIT], res[3][:, 0:SPLIT])
+        nc.scalar.copy(out_planes[:, 3, SPLIT:S], res[3][:, SPLIT:S])
 
         o_w, o_s = weave_and_quantise("o", out_planes)
         out_words = out_1[0].rearrange("p c r -> p (c r)").bitcast(I32)

@@ -51,10 +51,10 @@ def tile_picked_fkcdputbbiglift_none_po_kernel(
             for q in range(QUADS):
                 queues[q].dma_start(tile[32 * q : 32 * q + 4, :].bitcast(I32), src[0, 4 * q : 4 * q + 4, :].bitcast(I32))
 
-        def deal(engine, tile, src):
-            engine.tensor_copy(
-                out=tile[:].rearrange("p (t m) -> p t m", t=PACK),
-                in_=src.rearrange("p (m t) -> p t m", t=PACK),
+        def deal(tile, src, run):
+            nc.vector.tensor_copy(
+                out=tile[:].rearrange("p (t c i) -> p c t i", t=PACK, i=run),
+                in_=src.rearrange("p (c i t) -> p c t i", t=PACK, i=run),
             )
             return tile
 
@@ -79,13 +79,14 @@ def tile_picked_fkcdputbbiglift_none_po_kernel(
                 planes[:, :, lo:hi].rearrange("p t (c i) -> p c t i", i=4),
             )
 
-        def weave_and_quantise(name, planes):
+        def weave_and_quantise(name, planes, split):
             woven = sb(name + "_woven", [P, PACK * S], BF16)
             words = sb(name + "_words", [P, S], I32)
             scales = sb(name + "_scales", [P, S], U8)
-            weave(nc.scalar.copy, woven, planes, SPLIT, S)
+            if split < S:
+                weave(nc.scalar.copy, woven, planes, split, S)
             weave(nc.vector.tensor_copy, woven, planes, 0, W)
-            weave(nc.vector.tensor_copy, woven, planes, W, SPLIT)
+            weave(nc.vector.tensor_copy, woven, planes, W, split)
             for h in range(2):
                 nc.vector.quantize_mx(
                     out=words[:, W * h : W * (h + 1)].bitcast(FP8X4), scales=scales[:, W * h : W * (h + 1)],
@@ -112,11 +113,11 @@ def tile_picked_fkcdputbbiglift_none_po_kernel(
         load_scale_rows(xs, x_scales, [nc.sync] * QUADS)
         xw = load_words("xw", x_words, T)
         load_scale_rows(w1s_raw, w1_scales, [nc.sync] * QUADS)
+        w2w_raw = load_words("w2w_raw", w2_words, S)
         n2_l = load_list("n2_l", n2)
         n3_l = load_list("n3_l", n3)
-        n1_l = load_list("n1_l", n1)
-        w2w_raw = load_words("w2w_raw", w2_words, S)
         load_scale_rows(w2s_raw, w2_scales, [nc.sync] * QUADS)
+        n1_l = load_list("n1_l", n1)
         gn_c = sb("gn_c", [P, PACK], F32)
         nc.sync.dma_start(gn_c[:], gn.rearrange("(p t) o -> p (t o)", t=PACK))
         gs_c = sb("gs_c", [P, PACK], F32)
@@ -129,8 +130,8 @@ def tile_picked_fkcdputbbiglift_none_po_kernel(
         xc_s_raw = sb("xc_s_raw", [P, S], U8)
         nc.vector.tensor_copy(xc_s_raw[:], xs[:].indirect(cand_l[:]))
         xq_w = sb("xq_w", [P, S], U32)
-        w1w = deal(nc.vector, sb("w1w", [P, S], I32), w1w_raw[:])
-        w1s = deal(nc.vector, sb("w1s", [P, S], U8), w1s_raw[:])
+        w1w = deal(sb("w1w", [P, S], I32), w1w_raw[:], 4)
+        w1s = deal(sb("w1s", [P, S], U8), w1s_raw[:], 16)
         for h in range(2):
             nc.vector.tensor_copy(xq_w[:, HALVES[h]], xw[:].bitcast(U32).indirect(offs_l[:, 16 * h : 16 * (h + 1)]))
 
@@ -145,8 +146,8 @@ def tile_picked_fkcdputbbiglift_none_po_kernel(
 
         xc_w_raw = reuse.tile([P, S], U32, name="xc_w_raw", offset=4096, align_bytes=64)
         nc.vector.tensor_copy(xc_w_raw[:], xw[:].bitcast(U32).indirect(cand_l[:]))
-        w2w = deal(nc.vector, sb("w2w", [P, S], I32), w2w_raw[:])
-        w2s = deal(nc.vector, sb("w2s", [P, S], U8), w2s_raw[:])
+        w2w = deal(sb("w2w", [P, S], I32), w2w_raw[:], 4)
+        w2s = deal(sb("w2s", [P, S], U8), w2s_raw[:], 16)
 
         z_planes = sb("z_planes", [P, PACK, S], BF16)
         z2_planes = sb("z2_planes", [P, PACK, S], BF16)
@@ -198,21 +199,20 @@ def tile_picked_fkcdputbbiglift_none_po_kernel(
         put_difference(1)
         put_larger(0, part(rb01, 0))
         put_larger(1, part(rb01, 1))
-        neighbour_max(0)
         fetch_y(2)
-        neighbour_max(1)
+        neighbour_max(0)
         fetch_y(3)
-        neighbour_max(2)
+        for t in range(1, PACK):
+            neighbour_max(t)
         fetch_pairs(2)
         rb2 = sb("rb2", [P, W], F32)
         pair_max(rb2, 2, 1)
         put_difference(2)
-        neighbour_max(3)
+        for t in range(PACK):
+            round_z(t)
         fetch_pairs(3)
         put_difference(3)
         put_larger(2, rb2[:])
-        for t in range(PACK):
-            round_z(t)
 
         z_woven = reuse.tile([P, PACK * S], BF16, name="z_woven", offset=0, align_bytes=64)
         weave(nc.scalar.copy, z_woven, z_planes, 0, S)
@@ -222,8 +222,8 @@ def tile_picked_fkcdputbbiglift_none_po_kernel(
             product(banks_a[t], w2w, w2s, z_w, z_s, t)
         rb3 = reuse.tile([P, W], F32, name="rb3", offset=0, align_bytes=64)
         pair_max(rb3, 3, 1)
-        xc_w = deal(nc.vector, reuse.tile([P, S], I32, name="xc_w", offset=1024, align_bytes=64), xc_w_raw[:].bitcast(I32))
-        xc_s = deal(nc.vector, reuse.tile([P, S], U8, name="xc_s", offset=3072, align_bytes=64), xc_s_raw[:])
+        xc_w = deal(reuse.tile([P, S], I32, name="xc_w", offset=1024, align_bytes=64), xc_w_raw[:].bitcast(I32), 4)
+        xc_s = deal(reuse.tile([P, S], U8, name="xc_s", offset=3072, align_bytes=64), xc_s_raw[:], 16)
         put_larger(3, rb3[:])
         for t in range(PACK - 1):
             round_z2(t)
@@ -233,57 +233,70 @@ def tile_picked_fkcdputbbiglift_none_po_kernel(
         res = []
         a_part = [sb(f"a_part{t}", [P, W], F32) for t in range(PACK)]
 
+        b = {}
+        b_part = [sb(f"b_part{t}", [P, W], F32) for t in range(PACK)]
+
         def fetch_a(t):
             res.append(sb(f"res{t}", [P, S], F32, tag="b1" if t == 3 else None))
             nc.scalar.copy(res[t][:], banks_a[t][:])
+
+        def pick_a(t):
             nc.scalar.activation(a_part[t][:], res[t][:].indirect(n4_l[:]), COPY, scale=-0.5)
 
-        def put(t, b_part):
-            nc.vector.tensor_tensor(res[t][:].indirect(n4_l[:]), b_part[:], a_part[t][:], ALU.add)
+        def fetch_b(t):
+            b[t] = sb(f"b{t}", [P, S], F32)
+            nc.scalar.activation(b[t][:], banks_b[t][:], COPY, scale=0.0625)
+
+        def pick_b(t):
+            nc.scalar.activation(b_part[t][:], b[t][:].indirect(n5_l[:]), COPY)
+
+        def put(t):
+            nc.vector.tensor_tensor(res[t][:].indirect(n4_l[:]), b_part[t][:], a_part[t][:], ALU.add)
             if t < 2:
                 nc.sync.dma_start(out_planes[:, t, :], res[t][:])
             nc.sync.dma_start(out_rows[:, t, :], res[t][:])
 
-        def fetch_b(t):
-            b = sb(f"b{t}", [P, S], F32)
-            b_part = sb(f"b_part{t}", [P, W], F32)
-            nc.scalar.activation(b[:], banks_b[t][:], COPY, scale=0.0625)
-            nc.scalar.activation(b_part[:], b[:].indirect(n5_l[:]), COPY)
-            return b_part
-
         fetch_a(0)
         fetch_a(1)
-        nc.vector.tensor_scalar(z2_planes[:, 3, 0:SPLIT], dt[3][:, 0:SPLIT], gs_c[:, 3:4], None, ALU.mult)
-        nc.scalar.activation(z2_planes[:, 3, SPLIT:S], dt[3][:, SPLIT:S], COPY, scale=gs_c[:, 3:4])
-        z2_w, z2_s = weave_and_quantise("z2", z2_planes)
+        pick_a(0)
         fetch_a(2)
+        pick_a(1)
+        nc.vector.tensor_scalar(z2_planes[:, 3, :], dt[3][:], gs_c[:, 3:4], None, ALU.mult)
+        z2_w, z2_s = weave_and_quantise("z2", z2_planes, S)
 
-        b0 = sb("b0", [P, S], F32)
+        b[0] = sb("b0", [P, S], F32)
         for h in range(2):
             bank = psum.tile([P, W], F32, name=f"b0_{h}", tag=f"bank{h + 1}")
             product(bank, xc_w, xc_s, z2_w, z2_s, 0, HALVES[h])
             if h == 0:
-                nc.scalar.activation(b0[:, HALVES[h]], bank[:], COPY, scale=0.0625)
+                nc.scalar.activation(b[0][:, HALVES[h]], bank[:], COPY, scale=0.0625)
             else:
-                nc.vector.tensor_scalar(b0[:, HALVES[h]], bank[:], 0.0625, None, ALU.mult)
+                nc.vector.tensor_scalar(b[0][:, HALVES[h]], bank[:], 0.0625, None, ALU.mult)
         banks_b = {t: psum.tile([P, S], F32, name=f"b{t}_bank", tag=f"bank{t + 2}") for t in range(1, PACK)}
         for t in range(1, PACK):
             product(banks_b[t], xc_w, xc_s, z2_w, z2_s, t)
-        b_part0 = sb("b_part0", [P, W], F32)
-        nc.scalar.activation(b_part0[:, 0:128], b0[:].indirect(n5_l[:, 0:8]), COPY)
-        nc.vector.tensor_copy(b_part0[:, 128:256], b0[:].indirect(n5_l[:, 8:16]))
-        put(0, b_part0)
-        put(1, fetch_b(1))
-        put(2, fetch_b(2))
+        pick_a(2)
+        nc.vector.tensor_copy(b_part[0][:], b[0][:].indirect(n5_l[:]))
+        put(0)
+        fetch_b(1)
+        fetch_b(2)
+        pick_b(1)
+        put(1)
         fetch_a(3)
-        put(3, fetch_b(3))
+        pick_b(2)
+        put(2)
+        fetch_b(3)
+        pick_a(3)
+        pick_b(3)
+        put(3)
         nc.scalar.copy(out_planes[:, 2, :], res[2][:])
         nc.vector.tensor_copy(out_planes[:, 3, 0:SPLIT], res[3][:, 0:SPLIT])
         nc.scalar.copy(out_planes[:, 3, SPLIT:S], res[3][:, SPLIT:S])
 
-        o_w, o_s = weave_and_quantise("o", out_planes)
+        o_w, o_s = weave_and_quantise("o", out_planes, SPLIT)
         out_words = out_1[0].rearrange("p c r -> p (c r)").bitcast(I32)
         for h in range(2):
             nc.sync.dma_start(out_words[:, HALVES[h]], o_w[:, HALVES[h]])
         for q in range(QUADS):
-            nc.scalar.dma_start(out_2[0, 4 * q : 4 * q + 4, :].bitcast(I32), o_s[32 * q : 32 * q + 4, :].bitcast(I32))
+            queue = nc.sync if q == QUADS - 1 else nc.scalar
+            queue.dma_start(out_2[0, 4 * q : 4 * q + 4, :].bitcast(I32), o_s[32 * q : 32 * q + 4, :].bitcast(I32))

from contextlib import ExitStack

import concourse.mybir as mybir

F32 = mybir.dt.float32
BF16 = mybir.dt.bfloat16
I32 = mybir.dt.int32
U32 = mybir.dt.uint32
U16 = mybir.dt.uint16
U8 = mybir.dt.uint8
FP8X4 = mybir.dt.float8_e4m3fn_x4
ALU = mybir.AluOpType
COPY = mybir.ActivationFunctionType.Copy

P = 128
PACK = 4
T = 2048
S = 512
W = 256
QUADS = 4
SPLIT = 320
HALVES = [slice(0, W), slice(W, S)]

FLOPS = 3 * 2 * 512 * 512 * 512


def tile_picked_fkcdputbbiglift_none_po_kernel(
    tc, x_words, x_scales, w1_words, w1_scales, gn, w2_words, w2_scales, gs,
    offs, n1, n2, n3, cand, n4, n5, out_0, out_1, out_2,
):
    nc = tc.nc
    with ExitStack() as ctx:
        keep = ctx.enter_context(tc.tile_pool(name="keep", bufs=1))
        reuse = ctx.enter_context(tc.tile_pool(name="reuse", bufs=1))
        psum = ctx.enter_context(tc.psum_pool(name="psum", bufs=1))

        def sb(name, shape, dtype, tag=None):
            return keep.tile(shape, dtype, name=name, tag=tag or name, align_bytes=64)

        def load_list(name, src):
            tile = sb(name, list(src.shape), U16)
            nc.sync.dma_start(tile[:], src)
            return tile

        def load_words(name, src, cols):
            tile = sb(name, [P, cols], I32)
            nc.sync.dma_start(tile[:], src[0].rearrange("p c r -> p (c r)").bitcast(I32))
            return tile

        def load_scale_rows(tile, src, queues):
            for q in range(QUADS):
                queues[q].dma_start(tile[32 * q : 32 * q + 4, :].bitcast(I32), src[0, 4 * q : 4 * q + 4, :].bitcast(I32))

        def deal(tile, src, run):
            nc.vector.tensor_copy(
                out=tile[:].rearrange("p (t c i) -> p c t i", t=PACK, i=run),
                in_=src.rearrange("p (c i t) -> p c t i", t=PACK, i=run),
            )
            return tile

        def product(bank, lhs_words, lhs_scales, rhs_words, rhs_scales, t, span=slice(0, S)):
            cols = slice(P * t, P * (t + 1))
            nc.tensor.matmul_mx(
                out=bank[:],
                lhsT=lhs_words[:, cols].bitcast(FP8X4), lhsT_scale=lhs_scales[:, cols],
                rhs=rhs_words[:, span].bitcast(FP8X4), rhs_scale=rhs_scales[:, span],
                start=True, stop=True,
            )

        def quantise(name, woven):
            words = sb(name + "_words", [P, S], I32)
            scales = sb(name + "_scales", [P, S], U8)
            nc.vector.quantize_mx(out=words[:].bitcast(FP8X4), scales=scales[:], in_=woven[:])
            return words, scales

        def weave(engine_copy, woven, planes, lo, hi):
            engine_copy(
                woven[:, PACK * lo : PACK * hi].rearrange("p (c i t) -> p c t i", i=4, t=PACK),
                planes[:, :, lo:hi].rearrange("p t (c i) -> p c t i", i=4),
            )

        def weave_and_quantise(name, planes, split):
            woven = sb(name + "_woven", [P, PACK * S], BF16)
            words = sb(name + "_words", [P, S], I32)
            scales = sb(name + "_scales", [P, S], U8)
            if split < S:
                weave(nc.scalar.copy, woven, planes, split, S)
            weave(nc.vector.tensor_copy, woven, planes, 0, W)
            weave(nc.vector.tensor_copy, woven, planes, W, split)
            for h in range(2):
                nc.vector.quantize_mx(
                    out=words[:, W * h : W * (h + 1)].bitcast(FP8X4), scales=scales[:, W * h : W * (h + 1)],
                    in_=woven[:, PACK * W * h : PACK * W * (h + 1)],
                )
            return words, scales

        def woven_view(tile):
            return tile[:].rearrange("p (c i t) -> p c t i", i=4, t=PACK)

        def planes_view(tile):
            return tile[:].rearrange("p t (c i) -> p c t i", i=4)

        xs = sb("xs", [P, T], U8)
        nc.gpsimd.memset(xs[:].bitcast(I32), 0)
        w1s_raw = reuse.tile([P, S], U8, name="w1s_raw", offset=4096, align_bytes=64)
        nc.gpsimd.memset(w1s_raw[:].bitcast(I32), 0)
        w2s_raw = sb("w2s_raw", [P, S], U8)
        nc.gpsimd.memset(w2s_raw[:].bitcast(I32), 0)

        offs_l = load_list("offs_l", offs)
        cand_l = load_list("cand_l", cand)
        w1w_raw = load_words("w1w_raw", w1_words, S)
        load_scale_rows(xs, x_scales, [nc.sync] * QUADS)
        xw = load_words("xw", x_words, T)
        load_scale_rows(w1s_raw, w1_scales, [nc.sync] * QUADS)
        w2w_raw = load_words("w2w_raw", w2_words, S)
        n2_l = load_list("n2_l", n2)
        n3_l = load_list("n3_l", n3)
        load_scale_rows(w2s_raw, w2_scales, [nc.sync] * QUADS)
        n1_l = load_list("n1_l", n1)
        gn_c = sb("gn_c", [P, PACK], F32)
        nc.sync.dma_start(gn_c[:], gn.rearrange("(p t) o -> p (t o)", t=PACK))
        gs_c = sb("gs_c", [P, PACK], F32)
        nc.sync.dma_start(gs_c[:], gs.rearrange("(p t) o -> p (t o)", t=PACK))
        n4_l = load_list("n4_l", n4)
        n5_l = load_list("n5_l", n5)

        xq_s = sb("xq_s", [P, S], U8)
        nc.vector.tensor_copy(xq_s[:], xs[:].indirect(offs_l[:]))
        xc_s_raw = sb("xc_s_raw", [P, S], U8)
        nc.vector.tensor_copy(xc_s_raw[:], xs[:].indirect(cand_l[:]))
        xq_w = sb("xq_w", [P, S], U32)
        w1w = deal(sb("w1w", [P, S], I32), w1w_raw[:], 4)
        w1s = deal(sb("w1s", [P, S], U8), w1s_raw[:], 16)
        for h in range(2):
            nc.vector.tensor_copy(xq_w[:, HALVES[h]], xw[:].bitcast(U32).indirect(offs_l[:, 16 * h : 16 * (h + 1)]))

        y = [sb(f"y{t}", [P, S], F32) for t in range(PACK)]
        for h in range(2):
            bank = psum.tile([P, W], F32, name=f"y0_{h}", tag=f"bank{h}")
            product(bank, w1w, w1s, xq_w, xq_s, 0, HALVES[h])
            nc.scalar.copy(y[0][:, HALVES[h]], bank[:])
        banks_y = {t: psum.tile([P, S], F32, name=f"y{t}_bank", tag=f"bank{t + 1}") for t in range(1, PACK)}
        for t in range(1, PACK):
            product(banks_y[t], w1w, w1s, xq_w, xq_s, t)

        xc_w_raw = reuse.tile([P, S], U32, name="xc_w_raw", offset=4096, align_bytes=64)
        nc.vector.tensor_copy(xc_w_raw[:], xw[:].bitcast(U32).indirect(cand_l[:]))
        w2w = deal(sb("w2w", [P, S], I32), w2w_raw[:], 4)
        w2s = deal(sb("w2s", [P, S], U8), w2s_raw[:], 16)

        z_planes = sb("z_planes", [P, PACK, S], BF16)
        z2_planes = sb("z2_planes", [P, PACK, S], BF16)
        dt = [sb(f"dt{t}", [P, S], F32) for t in range(PACK)]
        larger = sb("larger", [P, PACK, S], F32)
        neg_pa = sb("neg_pa", [P, PACK * W], F32)
        pb = sb("pb", [P, PACK * W], F32)

        def part(tile, t, count=1):
            return tile[:, W * t : W * (t + count)]

        def fetch_y(t):
            nc.scalar.copy(y[t][:], banks_y[t][:])

        def fetch_pairs(t):
            nc.scalar.activation(part(neg_pa, t), y[t][:].indirect(n2_l[:]), COPY, scale=-1.0)
            if t == 0:
                nc.vector.tensor_copy(part(pb, t), y[t][:].indirect(n3_l[:]))
            else:
                nc.scalar.activation(part(pb, t), y[t][:].indirect(n3_l[:]), COPY)

        def put_difference(t):
            nc.vector.tensor_tensor(dt[t][:].indirect(n2_l[:]), part(pb, t), part(neg_pa, t), ALU.add)

        def pair_max(rb, t, count):
            nc.vector.scalar_tensor_tensor(rb[:], part(neg_pa, t, count), -0.5, part(pb, t, count), ALU.mult, ALU.max)

        def put_larger(t, rb):
            nc.vector.tensor_copy(dt[t][:].indirect(n3_l[:]), rb)

        def neighbour_max(t):
            other = sb(f"other{t}", [P, S], F32)
            for h in range(2):
                nc.scalar.activation(other[:, HALVES[h]], y[t][:].indirect(n1_l[:, 16 * h : 16 * (h + 1)]), COPY)
            nc.vector.tensor_tensor(larger[:, t, :], y[t][:], other[:], ALU.max)

        def round_z(t):
            nc.scalar.activation(z_planes[:, t, :], larger[:, t, :], COPY, scale=gn_c[:, t : t + 1])

        def round_z2(t):
            nc.scalar.activation(z2_planes[:, t, :], dt[t][:], COPY, scale=gs_c[:, t : t + 1])

        fetch_pairs(0)
        put_difference(0)
        fetch_y(1)
        fetch_pairs(1)
        rb01 = sb("rb01", [P, 2 * W], F32)
        pair_max(rb01, 0, 2)
        put_difference(1)
        put_larger(0, part(rb01, 0))
        put_larger(1, part(rb01, 1))
        fetch_y(2)
        neighbour_max(0)
        fetch_y(3)
        for t in range(1, PACK):
            neighbour_max(t)
        fetch_pairs(2)
        rb2 = sb("rb2", [P, W], F32)
        pair_max(rb2, 2, 1)
        put_difference(2)
        for t in range(PACK):
            round_z(t)
        fetch_pairs(3)
        put_difference(3)
        put_larger(2, rb2[:])

        z_woven = reuse.tile([P, PACK * S], BF16, name="z_woven", offset=0, align_bytes=64)
        weave(nc.scalar.copy, z_woven, z_planes, 0, S)
        z_w, z_s = quantise("z", z_woven)
        banks_a = [psum.tile([P, S], F32, name=f"a{t}_bank", tag=f"bank{(t + 5) % 8}") for t in range(PACK)]
        for t in range(PACK):
            product(banks_a[t], w2w, w2s, z_w, z_s, t)
        rb3 = reuse.tile([P, W], F32, name="rb3", offset=0, align_bytes=64)
        pair_max(rb3, 3, 1)
        xc_w = deal(reuse.tile([P, S], I32, name="xc_w", offset=1024, align_bytes=64), xc_w_raw[:].bitcast(I32), 4)
        xc_s = deal(reuse.tile([P, S], U8, name="xc_s", offset=3072, align_bytes=64), xc_s_raw[:], 16)
        put_larger(3, rb3[:])
        for t in range(PACK - 1):
            round_z2(t)

        out_rows = out_0.rearrange("(p t) j -> p t j", t=PACK)
        out_planes = sb("out_planes", [P, PACK, S], F32)
        res = []
        a_part = [sb(f"a_part{t}", [P, W], F32) for t in range(PACK)]

        b = {}
        b_part = [sb(f"b_part{t}", [P, W], F32) for t in range(PACK)]

        def fetch_a(t):
            res.append(sb(f"res{t}", [P, S], F32, tag="b1" if t == 3 else None))
            nc.scalar.copy(res[t][:], banks_a[t][:])

        def pick_a(t):
            nc.scalar.activation(a_part[t][:], res[t][:].indirect(n4_l[:]), COPY, scale=-0.5)

        def fetch_b(t):
            b[t] = sb(f"b{t}", [P, S], F32)
            nc.scalar.activation(b[t][:], banks_b[t][:], COPY, scale=0.0625)

        def pick_b(t):
            nc.scalar.activation(b_part[t][:], b[t][:].indirect(n5_l[:]), COPY)

        def put(t):
            nc.vector.tensor_tensor(res[t][:].indirect(n4_l[:]), b_part[t][:], a_part[t][:], ALU.add)
            if t < 2:
                nc.sync.dma_start(out_planes[:, t, :], res[t][:])
            nc.sync.dma_start(out_rows[:, t, :], res[t][:])

        fetch_a(0)
        fetch_a(1)
        pick_a(0)
        fetch_a(2)
        pick_a(1)
        nc.vector.tensor_scalar(z2_planes[:, 3, :], dt[3][:], gs_c[:, 3:4], None, ALU.mult)
        z2_w, z2_s = weave_and_quantise("z2", z2_planes, S)

        b[0] = sb("b0", [P, S], F32)
        for h in range(2):
            bank = psum.tile([P, W], F32, name=f"b0_{h}", tag=f"bank{h + 1}")
            product(bank, xc_w, xc_s, z2_w, z2_s, 0, HALVES[h])
            if h == 0:
                nc.scalar.activation(b[0][:, HALVES[h]], bank[:], COPY, scale=0.0625)
            else:
                nc.vector.tensor_scalar(b[0][:, HALVES[h]], bank[:], 0.0625, None, ALU.mult)
        banks_b = {t: psum.tile([P, S], F32, name=f"b{t}_bank", tag=f"bank{t + 2}") for t in range(1, PACK)}
        for t in range(1, PACK):
            product(banks_b[t], xc_w, xc_s, z2_w, z2_s, t)
        pick_a(2)
        nc.vector.tensor_copy(b_part[0][:], b[0][:].indirect(n5_l[:]))
        put(0)
        fetch_b(1)
        fetch_b(2)
        pick_b(1)
        put(1)
        fetch_a(3)
        pick_b(2)
        put(2)
        fetch_b(3)
        pick_a(3)
        pick_b(3)
        put(3)
        nc.scalar.copy(out_planes[:, 2, :], res[2][:])
        nc.vector.tensor_copy(out_planes[:, 3, 0:SPLIT], res[3][:, 0:SPLIT])
        nc.scalar.copy(out_planes[:, 3, SPLIT:S], res[3][:, SPLIT:S])

        o_w, o_s = weave_and_quantise("o", out_planes, SPLIT)
        out_words = out_1[0].rearrange("p c r -> p (c r)").bitcast(I32)
        for h in range(2):
            nc.sync.dma_start(out_words[:, HALVES[h]], o_w[:, HALVES[h]])
        for q in range(QUADS):
            queue = nc.sync if q == QUADS - 1 else nc.scalar
            queue.dma_start(out_2[0, 4 * q : 4 * q + 4, :].bitcast(I32), o_s[32 * q : 32 * q + 4, :].bitcast(I32))
